import numpy as np
import ml_dtypes


def mxq(x, axis, fmt="e4m3"):
    dtype, down = {"e4m3": (ml_dtypes.float8_e4m3fn, 7), "e5m2": (ml_dtypes.float8_e5m2, 14)}[fmt]
    v = np.moveaxis(np.asarray(x, np.float32).astype(ml_dtypes.bfloat16).astype(np.float64), axis, -1)
    blocks = v.reshape(v.shape[:-1] + (-1, 32))
    amax = np.abs(blocks).max(-1, keepdims=True)
    byte = np.maximum(np.where(amax > 0, np.frexp(amax)[1] - 1 + 127, 0) - down, 1)
    scale = np.exp2(byte - 127.0)
    codes = (blocks / scale).astype(np.float32).astype(dtype).astype(np.float64)
    return np.moveaxis((codes * scale).reshape(v.shape), -1, axis)


WIDE = False


def mx_kscale(k):
    if not WIDE:
        return np.ones(k)
    levels = np.array([10, -10, 5, -5, 0])
    if k % 512:
        return np.exp2(np.random.permutation(np.resize(levels, k // 32))).repeat(32)
    a = np.empty((k // 512, 16))
    for p in range(k // 512):
        a[p, :8] = np.random.permutation(np.resize(levels, 8))
        for g in range(8):
            far = levels[np.abs(levels - a[p, g]) >= 10]
            a[p, g + 8] = far[np.random.randint(len(far))]
    return np.exp2(a.ravel()).repeat(32)


def f64(x):
    return np.asarray(x).astype(np.float64)


def striped8(idx):
    return np.asarray(idx).reshape(8, -1, 16).transpose(0, 2, 1).reshape(128, -1).astype(np.uint16)


def unstriped8(offs):
    return offs.reshape(8, 16, -1).transpose(0, 2, 1).reshape(8, -1).astype(np.int64)


def pick8(x, idx, run):
    r = np.arange(len(x))
    return x[r[:, None], idx[r % (8 * run) // run]]


E2M1 = np.array([0.0, 0.5, 1.0, 1.5, 2.0, 3.0, 4.0, 6.0, -0.0, -0.5, -1.0, -1.5, -2.0, -3.0, -4.0, -6.0])


def pack_weight(w, fmt):
    k, n = w.shape
    w = f64(np.asarray(w, np.float32).astype(ml_dtypes.bfloat16)).reshape(k // 32, 32, n)
    amax = np.abs(w).max(1)
    if fmt == "e4m3":
        byte = np.frexp(amax)[1] - 1 + 127 - 7
    else:
        mant, ex = np.frexp(amax / 6.0)
        byte = np.where(mant > 0.5, ex, ex - 1) + 127
    byte = np.clip(np.where(amax > 0, byte, 1), 1, 254)
    scaled = (w * np.exp2(127.0 - byte)[:, None, :]).reshape(k, n).astype(np.float32)
    by_word = np.ascontiguousarray(scaled.reshape(k // 512, 128, 4, n).transpose(0, 1, 3, 2))
    if fmt == "e4m3":
        words = by_word.astype(ml_dtypes.float8_e4m3fn).view(np.uint8)
    else:
        c = by_word.astype(ml_dtypes.float4_e2m1fn).view(np.uint8) & 0xF
        words = (c[..., 0::2] | (c[..., 1::2] << 4)).reshape(k // 512, 128, 2 * n)
    return np.ascontiguousarray(words), np.ascontiguousarray(byte.astype(np.uint8).reshape(k // 512, 16, n))


def unpack_weight(words, scales, fmt):
    g, _, n = scales.shape
    words = np.ascontiguousarray(words).reshape(g, 128, n, -1)
    if fmt == "e4m3":
        vals = words.view(ml_dtypes.float8_e4m3fn).astype(np.float64)
    else:
        nib = np.empty((g, 128, n, 4), np.uint8)
        nib[..., 0::2] = words & 0xF
        nib[..., 1::2] = words >> 4
        vals = E2M1[nib]
    vals = vals * np.repeat(np.exp2(scales.astype(np.float64) - 127.0), 8, axis=1)[..., None]
    return vals.transpose(0, 1, 3, 2).reshape(g * 512, n)


D, T, U, X, I, J, Q = 512, 1024, 1024, 1024, 512, 256, 128


def setup_inputs():
    n = np.random.standard_normal
    idx = np.stack([np.random.permutation(T)[:I] for _ in range(8)])
    idx2 = np.stack([np.random.permutation(U)[:I] for _ in range(8)])
    idx3 = np.stack([np.random.permutation(I)[:J] for _ in range(8)])
    idx4 = np.stack([np.random.permutation(X)[:J] for _ in range(8)])
    idx5 = np.stack([np.random.permutation(U)[:J] for _ in range(8)])
    idx6 = np.stack([np.random.permutation(X)[:I] for _ in range(8)])
    idx7 = np.stack([np.random.permutation(U)[:I] for _ in range(8)])
    fd = mx_kscale(D)
    cachep = pack_weight(n((D, T)) / fd[:, None], "e2m1")
    draftp = pack_weight(n((D, U)) / fd[:, None], "e4m3")
    archp = pack_weight(n((D, X)) / fd[:, None], "e2m1")
    return {
        "query": (n((D, Q)) * 1.0 / np.sqrt(D) * fd[:, None]).astype(np.float32),
        "cache_words": cachep[0],
        "cache_scales": cachep[1],
        "draft_words": draftp[0],
        "draft_scales": draftp[1],
        "arch_words": archp[0],
        "arch_scales": archp[1],
        "offs": striped8(idx),
        "offs2": striped8(idx2),
        "offs3": striped8(idx3),
        "offs4": striped8(idx4),
        "offs5": striped8(idx5),
        "offs6": striped8(idx6),
        "offs7": striped8(idx7),
    }


def reference(query, cache_words, cache_scales, draft_words, draft_scales, arch_words, arch_scales, offs, offs2, offs3, offs4, offs5, offs6, offs7):
    idx = unstriped8(offs)
    idx2 = unstriped8(offs2)
    idx3 = unstriped8(offs3)
    idx4 = unstriped8(offs4)
    idx5 = unstriped8(offs5)
    idx6 = unstriped8(offs6)
    idx7 = unstriped8(offs7)
    cacheu = unpack_weight(cache_words, cache_scales, "e2m1")
    draftu = unpack_weight(draft_words, draft_scales, "e4m3")
    archu = unpack_weight(arch_words, arch_scales, "e2m1")
    queryq = mxq(f64(query), 0, "e4m3")
    a = queryq.T @ cacheu
    b = queryq.T @ draftu
    c0 = queryq.T @ archu
    w = pick8(a, idx, 16) + pick8(b, idx2, 16)
    v = pick8(w, idx3, 16) * 1.5
    f1 = np.zeros((Q, X))
    f1[np.arange(Q)[:, None], idx4[np.arange(Q) % 128 // 16]] = v
    f2 = np.zeros((Q, U))
    f2[np.arange(Q)[:, None], idx5[np.arange(Q) % 128 // 16]] = v
    cc = c0 - f1
    bb = np.maximum(b, f2)
    y = pick8(cc, idx6, 16) + pick8(bb, idx7, 16)
    return y

@@ -1,0 +1,152 @@
+from contextlib import ExitStack
+
+import concourse.mybir as mybir
+
+D, T, SLOTS, PICKS, Q = 512, 1024, 512, 256, 128
+FLOPS = 2 * D * Q * 3 * T
+
+F32 = mybir.dt.float32
+BF16 = mybir.dt.bfloat16
+I32 = mybir.dt.int32
+U32 = mybir.dt.uint32
+U16 = mybir.dt.uint16
+U8 = mybir.dt.uint8
+FP8X4 = mybir.dt.float8_e4m3fn_x4
+FP4X4 = mybir.dt.float4_e2m1fn_x4
+ADD = mybir.AluOpType.add
+SUB = mybir.AluOpType.subtract
+MULT = mybir.AluOpType.mult
+MAX = mybir.AluOpType.max
+COPY = mybir.ActivationFunctionType.Copy
+
+P = 128
+PACK = 4
+BANK = 512
+GROUP = 16
+
+
+def tile_attend_slotpages_three_kernel(
+    tc, query, cache_words, cache_scales, draft_words, draft_scales, arch_words, arch_scales,
+    offs, offs2, offs3, offs4, offs5, offs6, offs7, out,
+):
+    nc = tc.nc
+    with ExitStack() as ctx:
+        sb = ctx.enter_context(tc.tile_pool(name="sb", bufs=1))
+        psum = ctx.enter_context(tc.psum_pool(name="psum", bufs=1))
+
+        def load_list(name, src):
+            tile = sb.tile(list(src.shape), U16, name=name)
+            nc.sync.dma_start(tile[:], src)
+            return tile
+
+        def load_plane(name, src, queue):
+            plane = sb.tile([P, T], U8, name=name, align_bytes=64)
+            for quad in range(4):
+                queue.dma_start(
+                    plane[32 * quad : 32 * quad + 4, :].bitcast(I32),
+                    src[0, 4 * quad : 4 * quad + 4, :].bitcast(I32),
+                )
+            return plane
+
+        def load_words(name, src, width):
+            words = sb.tile([P, width], U8, name=name, align_bytes=64)
+            nc.sync.dma_start(words[:].bitcast(I32), src.bitcast(I32))
+            return words
+
+        q_raw = sb.tile([P, PACK, Q], F32, name="q_raw")
+        nc.sync.dma_start(q_raw[:], query.rearrange("(p j) q -> p j q", j=PACK))
+        cache_plane = load_plane("cache_plane", cache_scales, nc.sync)
+        cache_sb = load_words("cache_sb", cache_words[0], 2 * T)
+        draft_sb = load_words("draft_sb", draft_words[0].rearrange("p n t -> p (n t)"), 4 * T)
+        draft_plane = load_plane("draft_plane", draft_scales, nc.sync)
+        l1 = load_list("l1", offs)
+        l2 = load_list("l2", offs2)
+        l3 = load_list("l3", offs3)
+        l5 = load_list("l5", offs5)
+        l4 = load_list("l4", offs4)
+        arch_sb = load_words("arch_sb", arch_words[0], 2 * T)
+        arch_plane = load_plane("arch_plane", arch_scales, nc.sync)
+        l7 = load_list("l7", offs7)
+        l6 = load_list("l6", offs6)
+
+        f1 = sb.tile([P, T], F32, name="f1")
+        f2 = sb.tile([P, T], F32, name="f2")
+        nc.vector.memset(f2[:], 0.0)
+        nc.vector.memset(f1[:], 0.0)
+
+        q_bf = sb.tile([P, Q, PACK], BF16, name="q_bf", align_bytes=64)
+        nc.vector.tensor_copy(q_bf[:], q_raw[:].rearrange("p j q -> p q j"))
+        q_codes = sb.tile([P, Q], U32, name="q_codes", align_bytes=64)
+        q_plane = sb.tile([P, Q], U8, name="q_plane", align_bytes=64)
+        nc.vector.quantize_mx(
+            out=q_codes[:].bitcast(FP8X4), scales=q_plane[:], in_=q_bf[:].rearrange("p q j -> p (q j)")
+        )
+
+        def score(name, words, plane, dtype, word_bytes):
+            banks = []
+            for half in range(T // BANK):
+                bank = psum.tile([P, BANK], F32, name=name + str(half))
+                lo, hi = half * BANK, (half + 1) * BANK
+                nc.tensor.matmul_mx(
+                    out=bank[:],
+                    lhsT=q_codes[:].bitcast(FP8X4),
+                    lhsT_scale=q_plane[:],
+                    rhs=words[:, word_bytes * lo : word_bytes * hi].bitcast(dtype),
+                    rhs_scale=plane[:, lo:hi],
+                    start=True,
+                    stop=True,
+                )
+                banks.append(bank)
+            return banks
+
+        a_ps = score("a_ps", cache_sb, cache_plane, FP4X4, 2)
+        b_ps = score("b_ps", draft_sb, draft_plane, FP8X4, 4)
+        c_ps = score("c_ps", arch_sb, arch_plane, FP4X4, 2)
+
+        a = sb.tile([P, T], F32, name="a")
+        b = sb.tile([P, T], F32, name="b")
+        nc.scalar.activation(a[:, :BANK], a_ps[0][:], COPY)
+        nc.vector.tensor_copy(a[:, BANK:], a_ps[1][:])
+        nc.vector.tensor_copy(b[:, :BANK], b_ps[0][:])
+        nc.vector.tensor_copy(b[:, BANK:], b_ps[1][:])
+
+        half = SLOTS // 2
+        cols = half // GROUP
+        a_lo = sb.tile([P, half], F32, name="a_lo")
+        a_hi = sb.tile([P, half], F32, name="a_hi")
+        b_hi = sb.tile([P, half], F32, name="b_hi")
+        w = sb.tile([P, SLOTS], F32, name="w")
+        nc.scalar.activation(a_lo[:], a[:].indirect(l1[:, :cols]), COPY)
+        nc.scalar.activation(a_hi[:], a[:].indirect(l1[:, cols:]), COPY)
+        nc.vector.tensor_tensor(w[:, :half], b[:].indirect(l2[:, :cols]), a_lo[:], ADD)
+        nc.scalar.activation(b_hi[:], b[:].indirect(l2[:, cols:]), COPY)
+        nc.vector.tensor_tensor(w[:, half:], b_hi[:], a_hi[:], ADD)
+
+        vh = PICKS // 2
+        vcols = vh // GROUP
+        v = sb.tile([P, PICKS], F32, name="v")
+        nc.vector.tensor_scalar(v[:, :vh], w[:].indirect(l3[:, :vcols]), 1.5, 0.0, MULT, ADD)
+        nc.scalar.activation(v[:, vh:], w[:].indirect(l3[:, vcols:]), COPY, scale=1.5)
+
+        nc.scalar.activation(f2[:].indirect(l5[:]), v[:], COPY)
+        nc.scalar.activation(f1[:].indirect(l4[:]), v[:], COPY)
+
+        bb = sb.tile([P, T], F32, name="bb")
+        cc = sb.tile([P, T], F32, name="cc")
+        bb_lo = sb.tile([P, half], F32, name="bb_lo")
+        bb_hi = sb.tile([P, half], F32, name="bb_hi")
+        cc_hi = sb.tile([P, half], F32, name="cc_hi")
+        y_lo = sb.tile([P, half], F32, name="y_lo")
+        y_hi = sb.tile([P, half], F32, name="y_hi")
+        nc.vector.tensor_tensor(bb[:], b[:], f2[:], MAX)
+        nc.scalar.activation(bb_lo[:], bb[:].indirect(l7[:, :cols]), COPY)
+        nc.scalar.activation(bb_hi[:], bb[:].indirect(l7[:, cols:]), COPY)
+        for h in range(T // BANK):
+            nc.vector.tensor_tensor(
+                cc[:, h * BANK : (h + 1) * BANK], c_ps[h][:], f1[:, h * BANK : (h + 1) * BANK], SUB
+            )
+        nc.vector.tensor_tensor(y_lo[:], cc[:].indirect(l6[:, :cols]), bb_lo[:], ADD)
+        nc.scalar.activation(cc_hi[:], cc[:].indirect(l6[:, cols:]), COPY)
+        nc.sync.dma_start(out[:, :half], y_lo[:])
+        nc.vector.tensor_tensor(y_hi[:], cc_hi[:], bb_hi[:], ADD)
+        nc.scalar.dma_start(out[:, half:], y_hi[:])

@@ -55,10 +55,14 @@ def tile_attend_slotpages_three_kernel(
 
         q_raw = sb.tile([P, PACK, Q], F32, name="q_raw")
         nc.sync.dma_start(q_raw[:], query.rearrange("(p j) q -> p j q", j=PACK))
+        draft_plane = sb.tile([P, 4 * T], U8, name="draft_plane", align_bytes=64)
+        nc.sync.dma_start(
+            draft_plane[0:4, :].bitcast(I32).rearrange("r (quad c) -> r quad c", quad=4),
+            draft_scales[0].bitcast(I32).rearrange("(quad r) c -> r quad c", quad=4),
+        )
         cache_plane = load_plane("cache_plane", cache_scales, nc.sync)
         cache_sb = load_words("cache_sb", cache_words[0], 2 * T)
         draft_sb = load_words("draft_sb", draft_words[0].rearrange("p n t -> p (n t)"), 4 * T)
-        draft_plane = load_plane("draft_plane", draft_scales, nc.sync)
         l1 = load_list("l1", offs)
         l2 = load_list("l2", offs2)
         l3 = load_list("l3", offs3)
@@ -75,18 +79,32 @@ def tile_attend_slotpages_three_kernel(
         nc.vector.memset(f1[:], 0.0)
 
         q_bf = sb.tile([P, Q, PACK], BF16, name="q_bf", align_bytes=64)
-        nc.vector.tensor_copy(q_bf[:], q_raw[:].rearrange("p j q -> p q j"))
+        cut = Q // 2
+        nc.vector.tensor_copy(
+            q_bf[:, :cut, :].rearrange("p (c i) j -> p c j i", i=4),
+            q_raw[:, :, :cut].rearrange("p j (c i) -> p c j i", i=4),
+        )
+        nc.scalar.activation(
+            q_bf[:, cut:, :].rearrange("p (c i) j -> p c j i", i=4),
+            q_raw[:, :, cut:].rearrange("p j (c i) -> p c j i", i=4),
+            COPY,
+        )
         q_codes = sb.tile([P, Q], U32, name="q_codes", align_bytes=64)
         q_plane = sb.tile([P, Q], U8, name="q_plane", align_bytes=64)
         nc.vector.quantize_mx(
             out=q_codes[:].bitcast(FP8X4), scales=q_plane[:], in_=q_bf[:].rearrange("p q j -> p (q j)")
         )
 
-        def score(name, words, plane, dtype, word_bytes):
+        for quad in range(1, 4):
+            nc.vector.tensor_copy(
+                draft_plane[32 * quad : 32 * quad + 4, :T].bitcast(I32),
+                draft_plane[0:4, quad * T : (quad + 1) * T].bitcast(I32),
+            )
+
+        def score(name, words, plane, dtype, word_bytes, edges):
             banks = []
-            for half in range(T // BANK):
-                bank = psum.tile([P, BANK], F32, name=name + str(half))
-                lo, hi = half * BANK, (half + 1) * BANK
+            for lo, hi in zip(edges, edges[1:]):
+                bank = psum.tile([P, hi - lo], F32, name=name + str(lo))
                 nc.tensor.matmul_mx(
                     out=bank[:],
                     lhsT=q_codes[:].bitcast(FP8X4),
@@ -99,28 +117,27 @@ def tile_attend_slotpages_three_kernel(
                 banks.append(bank)
             return banks
 
-        a_ps = score("a_ps", cache_sb, cache_plane, FP4X4, 2)
-        b_ps = score("b_ps", draft_sb, draft_plane, FP8X4, 4)
-        c_ps = score("c_ps", arch_sb, arch_plane, FP4X4, 2)
+        a_ps = score("a_ps", cache_sb, cache_plane, FP4X4, 2, (0, 512, 768, 1024))
+        b_ps = score("b_ps", draft_sb, draft_plane, FP8X4, 4, (0, 512, 1024))
+        c_ps = score("c_ps", arch_sb, arch_plane, FP4X4, 2, (0, 512, 1024))
 
         a = sb.tile([P, T], F32, name="a")
         b = sb.tile([P, T], F32, name="b")
         nc.scalar.activation(a[:, :BANK], a_ps[0][:], COPY)
-        nc.vector.tensor_copy(a[:, BANK:], a_ps[1][:])
+        nc.vector.tensor_copy(a[:, 512:768], a_ps[1][:])
+        nc.scalar.activation(a[:, 768:], a_ps[2][:], COPY)
         nc.vector.tensor_copy(b[:, :BANK], b_ps[0][:])
         nc.vector.tensor_copy(b[:, BANK:], b_ps[1][:])
 
         half = SLOTS // 2
         cols = half // GROUP
-        a_lo = sb.tile([P, half], F32, name="a_lo")
-        a_hi = sb.tile([P, half], F32, name="a_hi")
+        a_g = sb.tile([P, SLOTS], F32, name="a_g")
         b_hi = sb.tile([P, half], F32, name="b_hi")
         w = sb.tile([P, SLOTS], F32, name="w")
-        nc.scalar.activation(a_lo[:], a[:].indirect(l1[:, :cols]), COPY)
-        nc.scalar.activation(a_hi[:], a[:].indirect(l1[:, cols:]), COPY)
-        nc.vector.tensor_tensor(w[:, :half], b[:].indirect(l2[:, :cols]), a_lo[:], ADD)
+        nc.scalar.activation(a_g[:], a[:].indirect(l1[:]), COPY)
+        nc.vector.tensor_tensor(w[:, :half], b[:].indirect(l2[:, :cols]), a_g[:, :half], ADD)
         nc.scalar.activation(b_hi[:], b[:].indirect(l2[:, cols:]), COPY)
-        nc.vector.tensor_tensor(w[:, half:], b_hi[:], a_hi[:], ADD)
+        nc.vector.tensor_tensor(w[:, half:], b_hi[:], a_g[:, half:], ADD)
 
         vh = PICKS // 2
         vcols = vh // GROUP
@@ -133,20 +150,18 @@ def tile_attend_slotpages_three_kernel(
 
         bb = sb.tile([P, T], F32, name="bb")
         cc = sb.tile([P, T], F32, name="cc")
-        bb_lo = sb.tile([P, half], F32, name="bb_lo")
-        bb_hi = sb.tile([P, half], F32, name="bb_hi")
+        bb_g = sb.tile([P, SLOTS], F32, name="bb_g")
         cc_hi = sb.tile([P, half], F32, name="cc_hi")
         y_lo = sb.tile([P, half], F32, name="y_lo")
         y_hi = sb.tile([P, half], F32, name="y_hi")
         nc.vector.tensor_tensor(bb[:], b[:], f2[:], MAX)
-        nc.scalar.activation(bb_lo[:], bb[:].indirect(l7[:, :cols]), COPY)
-        nc.scalar.activation(bb_hi[:], bb[:].indirect(l7[:, cols:]), COPY)
+        nc.scalar.activation(bb_g[:], bb[:].indirect(l7[:]), COPY)
         for h in range(T // BANK):
             nc.vector.tensor_tensor(
                 cc[:, h * BANK : (h + 1) * BANK], c_ps[h][:], f1[:, h * BANK : (h + 1) * BANK], SUB
             )
-        nc.vector.tensor_tensor(y_lo[:], cc[:].indirect(l6[:, :cols]), bb_lo[:], ADD)
+        nc.vector.tensor_tensor(y_lo[:], cc[:].indirect(l6[:, :cols]), bb_g[:, :half], ADD)
         nc.scalar.activation(cc_hi[:], cc[:].indirect(l6[:, cols:]), COPY)
         nc.sync.dma_start(out[:, :half], y_lo[:])
-        nc.vector.tensor_tensor(y_hi[:], cc_hi[:], bb_hi[:], ADD)
+        nc.vector.tensor_tensor(y_hi[:], cc_hi[:], bb_g[:, half:], ADD)
         nc.scalar.dma_start(out[:, half:], y_hi[:])

@@ -55,14 +55,15 @@ def tile_attend_slotpages_three_kernel(
 
         q_raw = sb.tile([P, PACK, Q], F32, name="q_raw")
         nc.sync.dma_start(q_raw[:], query.rearrange("(p j) q -> p j q", j=PACK))
-        draft_plane = sb.tile([P, 4 * T], U8, name="draft_plane", align_bytes=64)
-        nc.sync.dma_start(
-            draft_plane[0:4, :].bitcast(I32).rearrange("r (quad c) -> r quad c", quad=4),
-            draft_scales[0].bitcast(I32).rearrange("(quad r) c -> r quad c", quad=4),
-        )
         cache_plane = load_plane("cache_plane", cache_scales, nc.sync)
         cache_sb = load_words("cache_sb", cache_words[0], 2 * T)
         draft_sb = load_words("draft_sb", draft_words[0].rearrange("p n t -> p (n t)"), 4 * T)
+        draft_plane = sb.tile([P, BANK], U8, name="draft_plane", align_bytes=64)
+        for quad in range(4):
+            nc.sync.dma_start(
+                draft_plane[32 * quad + 4 : 32 * quad + 12, :].bitcast(I32),
+                draft_scales[0, 4 * quad : 4 * quad + 4, :].bitcast(I32).rearrange("r (h c) -> h r c", h=2),
+            )
         l1 = load_list("l1", offs)
         l2 = load_list("l2", offs2)
         l3 = load_list("l3", offs3)
@@ -79,29 +80,14 @@ def tile_attend_slotpages_three_kernel(
         nc.vector.memset(f1[:], 0.0)
 
         q_bf = sb.tile([P, Q, PACK], BF16, name="q_bf", align_bytes=64)
-        cut = Q // 2
-        nc.vector.tensor_copy(
-            q_bf[:, :cut, :].rearrange("p (c i) j -> p c j i", i=4),
-            q_raw[:, :, :cut].rearrange("p j (c i) -> p c j i", i=4),
-        )
-        nc.scalar.activation(
-            q_bf[:, cut:, :].rearrange("p (c i) j -> p c j i", i=4),
-            q_raw[:, :, cut:].rearrange("p j (c i) -> p c j i", i=4),
-            COPY,
-        )
+        nc.vector.tensor_copy(q_bf[:], q_raw[:].rearrange("p j q -> p q j"))
         q_codes = sb.tile([P, Q], U32, name="q_codes", align_bytes=64)
         q_plane = sb.tile([P, Q], U8, name="q_plane", align_bytes=64)
         nc.vector.quantize_mx(
             out=q_codes[:].bitcast(FP8X4), scales=q_plane[:], in_=q_bf[:].rearrange("p q j -> p (q j)")
         )
 
-        for quad in range(1, 4):
-            nc.vector.tensor_copy(
-                draft_plane[32 * quad : 32 * quad + 4, :T].bitcast(I32),
-                draft_plane[0:4, quad * T : (quad + 1) * T].bitcast(I32),
-            )
-
-        def score(name, words, plane, dtype, word_bytes, edges):
+        def score(name, words, scales_of, dtype, word_bytes, edges):
             banks = []
             for lo, hi in zip(edges, edges[1:]):
                 bank = psum.tile([P, hi - lo], F32, name=name + str(lo))
@@ -110,16 +96,16 @@ def tile_attend_slotpages_three_kernel(
                     lhsT=q_codes[:].bitcast(FP8X4),
                     lhsT_scale=q_plane[:],
                     rhs=words[:, word_bytes * lo : word_bytes * hi].bitcast(dtype),
-                    rhs_scale=plane[:, lo:hi],
+                    rhs_scale=scales_of(lo, hi),
                     start=True,
                     stop=True,
                 )
                 banks.append(bank)
             return banks
 
-        a_ps = score("a_ps", cache_sb, cache_plane, FP4X4, 2, (0, 512, 768, 1024))
-        b_ps = score("b_ps", draft_sb, draft_plane, FP8X4, 4, (0, 512, 1024))
-        c_ps = score("c_ps", arch_sb, arch_plane, FP4X4, 2, (0, 512, 1024))
+        a_ps = score("a_ps", cache_sb, lambda lo, hi: cache_plane[:, lo:hi], FP4X4, 2, (0, 512, 768, 1024))
+        b_ps = score("b_ps", draft_sb, lambda lo, hi: draft_plane[4 + 4 * (lo // BANK) :, :], FP8X4, 4, (0, 512, 1024))
+        c_ps = score("c_ps", arch_sb, lambda lo, hi: arch_plane[:, lo:hi], FP4X4, 2, (0, 512, 1024))
 
         a = sb.tile([P, T], F32, name="a")
         b = sb.tile([P, T], F32, name="b")

@@ -76,11 +76,13 @@ def tile_attend_slotpages_three_kernel(
 
         f1 = sb.tile([P, T], F32, name="f1")
         f2 = sb.tile([P, T], F32, name="f2")
-        nc.vector.memset(f2[:], 0.0)
-        nc.vector.memset(f1[:], 0.0)
+        nc.vector.memset(f2[:].bitcast(I32), 0)
+        nc.vector.memset(f1[:].bitcast(I32), 0)
 
         q_bf = sb.tile([P, Q, PACK], BF16, name="q_bf", align_bytes=64)
-        nc.vector.tensor_copy(q_bf[:], q_raw[:].rearrange("p j q -> p q j"))
+        cut = Q // 2
+        nc.vector.tensor_copy(q_bf[:, :cut, :], q_raw[:, :, :cut].rearrange("p j q -> p q j"))
+        nc.scalar.activation(q_bf[:, cut:, :], q_raw[:, :, cut:].rearrange("p j q -> p q j"), COPY)
         q_codes = sb.tile([P, Q], U32, name="q_codes", align_bytes=64)
         q_plane = sb.tile([P, Q], U8, name="q_plane", align_bytes=64)
         nc.vector.quantize_mx(

from contextlib import ExitStack

import concourse.mybir as mybir

D, T, SLOTS, PICKS, Q = 512, 1024, 512, 256, 128
FLOPS = 2 * D * Q * 3 * T

F32 = mybir.dt.float32
BF16 = mybir.dt.bfloat16
I32 = mybir.dt.int32
U32 = mybir.dt.uint32
U16 = mybir.dt.uint16
U8 = mybir.dt.uint8
FP8X4 = mybir.dt.float8_e4m3fn_x4
FP4X4 = mybir.dt.float4_e2m1fn_x4
ADD = mybir.AluOpType.add
SUB = mybir.AluOpType.subtract
MULT = mybir.AluOpType.mult
MAX = mybir.AluOpType.max
COPY = mybir.ActivationFunctionType.Copy

P = 128
PACK = 4
BANK = 512
GROUP = 16


def tile_attend_slotpages_three_kernel(
    tc, query, cache_words, cache_scales, draft_words, draft_scales, arch_words, arch_scales,
    offs, offs2, offs3, offs4, offs5, offs6, offs7, out,
):
    nc = tc.nc
    with ExitStack() as ctx:
        sb = ctx.enter_context(tc.tile_pool(name="sb", bufs=1))
        psum = ctx.enter_context(tc.psum_pool(name="psum", bufs=1))

        def load_list(name, src):
            tile = sb.tile(list(src.shape), U16, name=name)
            nc.sync.dma_start(tile[:], src)
            return tile

        def load_plane(name, src, queue):
            plane = sb.tile([P, T], U8, name=name, align_bytes=64)
            for quad in range(4):
                queue.dma_start(
                    plane[32 * quad : 32 * quad + 4, :].bitcast(I32),
                    src[0, 4 * quad : 4 * quad + 4, :].bitcast(I32),
                )
            return plane

        def load_words(name, src, width):
            words = sb.tile([P, width], U8, name=name, align_bytes=64)
            nc.sync.dma_start(words[:].bitcast(I32), src.bitcast(I32))
            return words

        q_raw = sb.tile([P, PACK, Q], F32, name="q_raw")
        nc.sync.dma_start(q_raw[:], query.rearrange("(p j) q -> p j q", j=PACK))
        cache_plane = load_plane("cache_plane", cache_scales, nc.sync)
        cache_sb = load_words("cache_sb", cache_words[0], 2 * T)
        draft_sb = load_words("draft_sb", draft_words[0].rearrange("p n t -> p (n t)"), 4 * T)
        draft_plane = sb.tile([P, BANK], U8, name="draft_plane", align_bytes=64)
        for quad in range(4):
            nc.sync.dma_start(
                draft_plane[32 * quad + 4 : 32 * quad + 12, :].bitcast(I32),
                draft_scales[0, 4 * quad : 4 * quad + 4, :].bitcast(I32).rearrange("r (h c) -> h r c", h=2),
            )
        l1 = load_list("l1", offs)
        l2 = load_list("l2", offs2)
        l3 = load_list("l3", offs3)
        l5 = load_list("l5", offs5)
        l4 = load_list("l4", offs4)
        arch_sb = load_words("arch_sb", arch_words[0], 2 * T)
        arch_plane = load_plane("arch_plane", arch_scales, nc.sync)
        l7 = load_list("l7", offs7)
        l6 = load_list("l6", offs6)

        f1 = sb.tile([P, T], F32, name="f1")
        f2 = sb.tile([P, T], F32, name="f2")
        nc.vector.memset(f2[:].bitcast(I32), 0)
        nc.vector.memset(f1[:].bitcast(I32), 0)

        q_bf = sb.tile([P, Q, PACK], BF16, name="q_bf", align_bytes=64)
        cut = Q // 2
        nc.vector.tensor_copy(q_bf[:, :cut, :], q_raw[:, :, :cut].rearrange("p j q -> p q j"))
        nc.scalar.activation(q_bf[:, cut:, :], q_raw[:, :, cut:].rearrange("p j q -> p q j"), COPY)
        q_codes = sb.tile([P, Q], U32, name="q_codes", align_bytes=64)
        q_plane = sb.tile([P, Q], U8, name="q_plane", align_bytes=64)
        nc.vector.quantize_mx(
            out=q_codes[:].bitcast(FP8X4), scales=q_plane[:], in_=q_bf[:].rearrange("p q j -> p (q j)")
        )

        def score(name, words, scales_of, dtype, word_bytes, edges):
            banks = []
            for lo, hi in zip(edges, edges[1:]):
                bank = psum.tile([P, hi - lo], F32, name=name + str(lo))
                nc.tensor.matmul_mx(
                    out=bank[:],
                    lhsT=q_codes[:].bitcast(FP8X4),
                    lhsT_scale=q_plane[:],
                    rhs=words[:, word_bytes * lo : word_bytes * hi].bitcast(dtype),
                    rhs_scale=scales_of(lo, hi),
                    start=True,
                    stop=True,
                )
                banks.append(bank)
            return banks

        a_ps = score("a_ps", cache_sb, lambda lo, hi: cache_plane[:, lo:hi], FP4X4, 2, (0, 512, 768, 1024))
        b_ps = score("b_ps", draft_sb, lambda lo, hi: draft_plane[4 + 4 * (lo // BANK) :, :], FP8X4, 4, (0, 512, 1024))
        c_ps = score("c_ps", arch_sb, lambda lo, hi: arch_plane[:, lo:hi], FP4X4, 2, (0, 512, 1024))

        a = sb.tile([P, T], F32, name="a")
        b = sb.tile([P, T], F32, name="b")
        nc.scalar.activation(a[:, :BANK], a_ps[0][:], COPY)
        nc.vector.tensor_copy(a[:, 512:768], a_ps[1][:])
        nc.scalar.activation(a[:, 768:], a_ps[2][:], COPY)
        nc.vector.tensor_copy(b[:, :BANK], b_ps[0][:])
        nc.vector.tensor_copy(b[:, BANK:], b_ps[1][:])

        half = SLOTS // 2
        cols = half // GROUP
        a_g = sb.tile([P, SLOTS], F32, name="a_g")
        b_hi = sb.tile([P, half], F32, name="b_hi")
        w = sb.tile([P, SLOTS], F32, name="w")
        nc.scalar.activation(a_g[:], a[:].indirect(l1[:]), COPY)
        nc.vector.tensor_tensor(w[:, :half], b[:].indirect(l2[:, :cols]), a_g[:, :half], ADD)
        nc.scalar.activation(b_hi[:], b[:].indirect(l2[:, cols:]), COPY)
        nc.vector.tensor_tensor(w[:, half:], b_hi[:], a_g[:, half:], ADD)

        vh = PICKS // 2
        vcols = vh // GROUP
        v = sb.tile([P, PICKS], F32, name="v")
        nc.vector.tensor_scalar(v[:, :vh], w[:].indirect(l3[:, :vcols]), 1.5, 0.0, MULT, ADD)
        nc.scalar.activation(v[:, vh:], w[:].indirect(l3[:, vcols:]), COPY, scale=1.5)

        nc.scalar.activation(f2[:].indirect(l5[:]), v[:], COPY)
        nc.scalar.activation(f1[:].indirect(l4[:]), v[:], COPY)

        bb = sb.tile([P, T], F32, name="bb")
        cc = sb.tile([P, T], F32, name="cc")
        bb_g = sb.tile([P, SLOTS], F32, name="bb_g")
        cc_hi = sb.tile([P, half], F32, name="cc_hi")
        y_lo = sb.tile([P, half], F32, name="y_lo")
        y_hi = sb.tile([P, half], F32, name="y_hi")
        nc.vector.tensor_tensor(bb[:], b[:], f2[:], MAX)
        nc.scalar.activation(bb_g[:], bb[:].indirect(l7[:]), COPY)
        for h in range(T // BANK):
            nc.vector.tensor_tensor(
                cc[:, h * BANK : (h + 1) * BANK], c_ps[h][:], f1[:, h * BANK : (h + 1) * BANK], SUB
            )
        nc.vector.tensor_tensor(y_lo[:], cc[:].indirect(l6[:, :cols]), bb_g[:, :half], ADD)
        nc.scalar.activation(cc_hi[:], cc[:].indirect(l6[:, cols:]), COPY)
        nc.sync.dma_start(out[:, :half], y_lo[:])
        nc.vector.tensor_tensor(y_hi[:], cc_hi[:], bb_g[:, half:], ADD)
        nc.scalar.dma_start(out[:, half:], y_hi[:])
